import numpy as np
import ml_dtypes


def mxq(x, axis, fmt="e4m3"):
    dtype, down = {"e4m3": (ml_dtypes.float8_e4m3fn, 7), "e5m2": (ml_dtypes.float8_e5m2, 14)}[fmt]
    v = np.moveaxis(np.asarray(x, np.float32).astype(ml_dtypes.bfloat16).astype(np.float64), axis, -1)
    blocks = v.reshape(v.shape[:-1] + (-1, 32))
    amax = np.abs(blocks).max(-1, keepdims=True)
    byte = np.maximum(np.where(amax > 0, np.frexp(amax)[1] - 1 + 127, 0) - down, 1)
    scale = np.exp2(byte - 127.0)
    codes = (blocks / scale).astype(np.float32).astype(dtype).astype(np.float64)
    return np.moveaxis((codes * scale).reshape(v.shape), -1, axis)


WIDE = False


def mx_kscale(k):
    if not WIDE:
        return np.ones(k)
    levels = np.array([10, -10, 5, -5, 0])
    if k % 512:
        return np.exp2(np.random.permutation(np.resize(levels, k // 32))).repeat(32)
    a = np.empty((k // 512, 16))
    for p in range(k // 512):
        a[p, :8] = np.random.permutation(np.resize(levels, 8))
        for g in range(8):
            far = levels[np.abs(levels - a[p, g]) >= 10]
            a[p, g + 8] = far[np.random.randint(len(far))]
    return np.exp2(a.ravel()).repeat(32)


def f64(x):
    return np.asarray(x).astype(np.float64)


def striped(idx):
    return np.tile(idx.reshape(-1, 16).T, (8, 1)).astype(np.uint16)


def unstriped(offs):
    return offs[:16].T.reshape(-1).astype(np.int64)


def pack_weight(w):
    k, n = w.shape
    w = f64(np.asarray(w, np.float32).astype(ml_dtypes.bfloat16)).reshape(k // 32, 32, n)
    amax = np.abs(w).max(1)
    byte = np.clip(np.where(amax > 0, np.frexp(amax)[1] - 1 + 127 - 7, 1), 1, 254)
    scaled = (w * np.exp2(127.0 - byte)[:, None, :]).reshape(k, n).astype(np.float32)
    words = np.ascontiguousarray(scaled.reshape(k // 512, 128, 4, n).transpose(0, 1, 3, 2)).astype(ml_dtypes.float8_e4m3fn).view(np.uint8)
    return words, np.ascontiguousarray(byte.astype(np.uint8).reshape(k // 512, 16, n))


def unpack_weight(words, scales):
    g, p, n, _ = words.shape
    vals = np.ascontiguousarray(words).view(ml_dtypes.float8_e4m3fn).astype(np.float64) * np.repeat(np.exp2(scales.astype(np.float64) - 127.0), 8, axis=1)[..., None]
    return vals.transpose(0, 1, 3, 2).reshape(g * 512, n)


K, T, S, N, H = 512, 2048, 512, 256, 512


def setup_inputs():
    n = np.random.standard_normal
    s = mx_kscale(K)[:, None]
    u = mx_kscale(H)
    packed_xT = pack_weight(n((K, T)) * s)
    return {
        "x_words": packed_xT[0],
        "x_scales": packed_xT[1],
        "w1": (n((K, H)) / np.sqrt(K) / s).astype(np.float32),
        "ef": (0.6 * n((H, S))).astype(np.float32),
        "unit": (np.random.uniform(0.6, 1.4, (H, 1)) * u[:, None]).astype(np.float32),
        "w2": (n((H, N)) / np.sqrt(H) / u[:, None]).astype(np.float32),
        "offs": striped(np.random.permutation(T)[:S]),
        "r1": striped(np.random.permutation(S)),
        "r2": striped(np.random.permutation(S)),
        "r3": striped(np.random.permutation(S)),
    }


def reference(x_words, x_scales, w1, ef, unit, w2, offs, r1, r2, r3):
    xq = unpack_weight(x_words, x_scales)[:, unstriped(offs)]
    y = mxq(f64(w1), 0, "e4m3").T @ xq
    a1 = y[:, unstriped(r1)]
    st1 = y + a1
    a2 = st1[:, unstriped(r2)]
    st2 = st1 + a2
    efk = f64(ef) + np.tanh(st2)
    a3 = efk[:, unstriped(r3)]
    st3 = st2 - (1.5 * a3)
    hid = f64(unit) * st3
    return mxq(f64(w2), 0, "e4m3").T @ mxq(hid, 0, "e4m3")

from contextlib import ExitStack

import concourse.mybir as mybir

K, T, S, N, H = 512, 2048, 512, 256, 512
FLOPS = 2 * K * H * S + 2 * H * N * S

F32 = mybir.dt.float32
BF16 = mybir.dt.bfloat16
I32 = mybir.dt.int32
U32 = mybir.dt.uint32
U16 = mybir.dt.uint16
U8 = mybir.dt.uint8
FP8X4 = mybir.dt.float8_e4m3fn_x4
MULT = mybir.AluOpType.mult
ADD = mybir.AluOpType.add
MIN = mybir.AluOpType.min
MAX = mybir.AluOpType.max
COPY = mybir.ActivationFunctionType.Copy
TANH = mybir.ActivationFunctionType.Tanh

P = 128
PACK = 4
LIST_COLS = S // 16
WINDOW = 704
HALF = S // 2
PARTS = ((0, 256), (256, 384), (384, 512))
BIG = 2.0**126


def tile_picked_yrecdbl_sum_p_kernel(
    tc, x_words, x_scales, w1, ef, unit, w2, offs, r1, r2, r3, out
):
    nc = tc.nc
    with ExitStack() as ctx:
        keep = ctx.enter_context(tc.tile_pool(name="keep", bufs=1))
        psum = ctx.enter_context(tc.psum_pool(name="psum", bufs=1))

        def sb(shape, dtype, name):
            return keep.tile(shape, dtype, name=name, align_bytes=64)

        def gather(on_vector, dst, window, offsets):
            if on_vector:
                nc.vector.tensor_copy(dst, window.indirect(offsets))
            else:
                nc.scalar.activation(dst, window.indirect(offsets), COPY)

        def entries(lst, cols):
            return lst[:, cols.start // 16 : cols.stop // 16]

        offs_sb = keep.tile([P, LIST_COLS], U16, name="offs_sb")
        r1_sb = keep.tile([P, LIST_COLS], U16, name="r1_sb")
        r2_sb = keep.tile([P, LIST_COLS], U16, name="r2_sb")
        r3_sb = keep.tile([P, LIST_COLS], U16, name="r3_sb")

        xs_all = sb([P, T], U8, "xs_all")
        xw_all = sb([P, T], U32, "xw_all")
        w1_raw = sb([P, PACK, H], F32, "w1_raw")
        w2_raw = sb([P, PACK, N], F32, "w2_raw")
        ef_raw = sb([P, PACK, S], F32, "ef_raw")
        unit_sb = sb([P, PACK], F32, "unit_sb")

        nc.vector.memset(xs_all[:].bitcast(I32), 0)

        nc.sync.dma_start(w1_raw[:], w1.rearrange("(p j) c -> p j c", j=PACK))
        nc.sync.dma_start(offs_sb[:], offs)
        for q in range(4):
            nc.sync.dma_start(
                xs_all[32 * q : 32 * q + 4, :].bitcast(I32),
                x_scales[0, 4 * q : 4 * q + 4, :].bitcast(I32),
            )
        nc.sync.dma_start(
            xw_all[:].bitcast(I32), x_words[0].rearrange("p c r -> p (c r)").bitcast(I32)
        )
        nc.sync.dma_start(unit_sb[:], unit.rearrange("(p t) o -> p (t o)", t=PACK))
        nc.sync.dma_start(r1_sb[:], r1)
        nc.sync.dma_start(ef_raw[:], ef.rearrange("(p t) s -> p t s", t=PACK))
        nc.sync.dma_start(r2_sb[:], r2)
        nc.sync.dma_start(r3_sb[:], r3)
        nc.sync.dma_start(w2_raw[:], w2.rearrange("(p j) c -> p j c", j=PACK))

        y = [sb([P, WINDOW], F32, f"y{t}") for t in range(PACK)]
        st1 = [sb([P, WINDOW], F32, f"st1_{t}") for t in range(PACK)]
        for tile in y + st1:
            nc.gpsimd.memset(tile[:, S:], 0.0)

        w1_bf = sb([P, PACK, P, PACK], BF16, "w1_bf")
        w1_src = w1_raw[:].rearrange("p j (m t) -> p m j t", t=PACK)
        w1_dst = w1_bf[:].rearrange("p t m j -> p m j t")
        split = 88
        nc.vector.tensor_copy(w1_dst[:, :split], w1_src[:, :split])
        nc.scalar.activation(w1_dst[:, split:], w1_src[:, split:], COPY)
        w1_codes = sb([P, H], U32, "w1_codes")
        w1_scales = sb([P, H], U8, "w1_scales")
        nc.vector.quantize_mx(
            out=w1_codes[:].bitcast(FP8X4),
            scales=w1_scales[:],
            in_=w1_bf[:].rearrange("p t m j -> p (t m j)"),
        )

        back = sb([P, PACK], F32, "back")
        inv_raw = sb([P, PACK], F32, "inv_raw")
        inv = sb([P, PACK], F32, "inv")
        nc.vector.tensor_scalar(back[:], unit_sb[:], -1.5, None, MULT)
        nc.vector.reciprocal(inv_raw[:], unit_sb[:])
        nc.vector.tensor_scalar(inv[:], inv_raw[:], BIG, -BIG, MIN, MAX)

        xs = sb([P, S], U8, "xs")
        nc.vector.tensor_copy(xs[:], xs_all[:].indirect(offs_sb[:]))
        halves = [slice(0, HALF), slice(HALF, S)]
        xw = [sb([P, HALF], U32, f"xw{h}") for h in range(2)]
        for h in range(2):
            nc.vector.tensor_copy(xw[h][:], xw_all[:].indirect(entries(offs_sb, halves[h])))

        y_ps = [psum.tile([P, S], F32, name=f"y_ps{t}") for t in range(PACK)]
        ef_s = [sb([P, S], F32, f"ef_s{t}") for t in range(PACK)]
        a1 = [sb([P, S], F32, f"a1_{t}") for t in range(PACK)]
        a2 = [sb([P, S], F32, f"a2_{t}") for t in range(PACK)]
        st2 = sb([P, PACK, S], F32, "st2")
        th = [sb([P, S], F32, f"th{t}") for t in range(PACK)]
        efk = [sb([P, S], F32, f"efk{t}") for t in range(PACK)]
        w2_bf = sb([P, N, PACK], BF16, "w2_bf")
        w2_codes = sb([P, N], U32, "w2_codes")
        w2_scales = sb([P, N], U8, "w2_scales")
        parts = [slice(a, b) for a, b in PARTS]
        a3_first = sb([P, PACK, HALF], F32, "a3_first")
        a3 = [a3_first[:]] + [
            tile[:].rearrange("p (t c) -> p t c", t=PACK) for tile in (th[3], ef_s[3])
        ]

        def M(t, h):
            cols = slice(t * P, (t + 1) * P)
            nc.tensor.matmul_mx(
                out=y_ps[t][:, halves[h]],
                lhsT=w1_codes[:, cols].bitcast(FP8X4),
                lhsT_scale=w1_scales[:, cols],
                rhs=xw[h][:].bitcast(FP8X4),
                rhs_scale=xs[:, halves[h]],
                start=True,
                stop=True,
            )

        def E(t, cols):
            if t in (0,):
                nc.vector.tensor_scalar(y[t][:, cols], y_ps[t][:, cols], unit_sb[:, t : t + 1], None, MULT)
            else:
                nc.scalar.activation(y[t][:, cols], y_ps[t][:, cols], COPY, scale=unit_sb[:, t : t + 1])

        def G1(t):
            gather(t in (0, 1), a1[t][:], y[t][:], r1_sb[:])

        def A1(t):
            nc.vector.scalar_tensor_tensor(
                st1[t][:, :S], y_ps[t][:], unit_sb[:, t : t + 1], a1[t][:], MULT, ADD
            )

        def G2(t):
            gather(t in (2,), a2[t][:], st1[t][:], r2_sb[:])

        def A2(t):
            nc.vector.tensor_tensor(st2[:, t, :], st1[t][:, :S], a2[t][:], ADD)

        def TH(t):
            nc.scalar.activation(th[t][:], st2[:, t, :], TANH, scale=inv[:, t : t + 1])

        def PRE(t):
            nc.gpsimd.tensor_scalar(ef_s[t][:], ef_raw[:, t, :], back[:, t : t + 1], 0.0, MULT, ADD)

        def FB(t):
            nc.vector.scalar_tensor_tensor(
                efk[t][:], th[t][:], back[:, t : t + 1], ef_s[t][:], MULT, ADD
            )

        def W():
            nc.gpsimd.tensor_scalar(
                w2_bf[:].rearrange("p (c i) j -> p c j i", i=4),
                w2_raw[:].rearrange("p j (c i) -> p c j i", i=4),
                1.0, 0.0, MULT, ADD,
            )

        def WQ():
            nc.vector.quantize_mx(
                out=w2_codes[:].bitcast(FP8X4),
                scales=w2_scales[:],
                in_=w2_bf[:].rearrange("p c j -> p (c j)"),
            )

        def G3(t, h):
            gather((t, h) in ((3, 0),), a3[h][:, t, :], efk[t][:], entries(r3_sb, parts[h]))

        def OUT(h):
            cols = parts[h]
            width = cols.stop - cols.start
            hid = sb([P, width, PACK], BF16, f"hid{h}")
            nc.vector.tensor_tensor(
                hid[:].rearrange("p (c i) t -> p c t i", i=4),
                st2[:, :, cols].rearrange("p t (c i) -> p c t i", i=4),
                a3[h].rearrange("p t (c i) -> p c t i", i=4),
                ADD,
            )
            hid_codes = sb([P, width], U32, f"hid_codes{h}")
            hid_scales = sb([P, width], U8, f"hid_scales{h}")
            nc.vector.quantize_mx(
                out=hid_codes[:].bitcast(FP8X4),
                scales=hid_scales[:],
                in_=hid[:].rearrange("p c t -> p (c t)"),
            )
            o_ps = psum.tile([P, 2, width], F32, name=f"o_ps{h}")
            for b in range(2):
                rows = slice(b * P, (b + 1) * P)
                nc.tensor.matmul_mx(
                    out=o_ps[:, b, :],
                    lhsT=w2_codes[:, rows].bitcast(FP8X4),
                    lhsT_scale=w2_scales[:, rows],
                    rhs=hid_codes[:].bitcast(FP8X4),
                    rhs_scale=hid_scales[:],
                    start=True,
                    stop=True,
                )
            o_sb = sb([P, 2, width], F32, f"o_sb{h}")
            if h in (2,):
                nc.vector.tensor_copy(o_sb[:], o_ps[:])
            else:
                nc.scalar.activation(o_sb[:], o_ps[:], COPY)
            nc.sync.dma_start(out.rearrange("(b p) s -> p b s", p=P)[:, :, cols], o_sb[:])

        for t, h in ((0, 0), (1, 0), (0, 1), (1, 1), (2, 0), (2, 1), (3, 0), (3, 1)):
            M(t, h)
        W()
        for t in range(PACK):
            PRE(t)
        for t in range(PACK):
            E(t, slice(0, S))
        for stage in (G1, A1, G2, A2, TH, FB):
            for t in range(PACK):
                stage(t)
        WQ()
        for h in range(len(parts)):
            for t in range(PACK):
                G3(t, h)
            OUT(h)
